import numpy as np, ml_dtypes
CORES = [211,219,227,235,243,251,83,91,99,107,115,123]
N = 12
NH, QP = 6, 64
def setup_inputs(rng):
    return {"q": rng.standard_normal((N, 128, NH * QP), dtype=np.float32).astype(ml_dtypes.bfloat16), "k": rng.standard_normal((N, 128, NH * 128), dtype=np.float32).astype(ml_dtypes.bfloat16), "v": rng.standard_normal((N, 128, NH * 128), dtype=np.float32).astype(ml_dtypes.bfloat16)}
def setup_inputs_big(rng):
    d = setup_inputs(rng)
    for k in ("q", "k", "v"): d[k] = (d[k].astype(np.float32) * 1024.0).astype(d[k].dtype)
    return d
def setup_inputs_small(rng):
    d = setup_inputs(rng)
    for k in ("q", "k", "v"): d[k] = (d[k].astype(np.float32) * (1 / 1024.0)).astype(d[k].dtype)
    return d
def setup_inputs_apart(rng):
    d = setup_inputs(rng)
    f = (10.0 ** rng.permutation(np.linspace(-1.5, 1.5, N))).astype(np.float32).reshape(N, 1, 1)
    for k in ("q", "k", "v"): d[k] = (d[k].astype(np.float32) * f).astype(d[k].dtype)
    return d
def reference(q, k, v):
    Q, K, V = q.astype(np.float64), k.astype(np.float64), v.astype(np.float64)
    y = np.zeros((N, 128, NH * QP))
    for r in range(N):
        for h in range(NH):
            for j in range(N):
                S = np.maximum(K[j][:, 128 * h:128 * h + 128].T @ Q[r][:, QP * h:QP * h + QP], 0.0)
                y[r][:, QP * h:QP * h + QP] += V[j][:, 128 * h:128 * h + 128].T @ S
    return {"y": y.astype(ml_dtypes.bfloat16 if q.dtype != np.float64 else np.float64)}

@@ -1,0 +1,192 @@
+from concourse.bass import DstId, RemoteDMATransfer
+from concourse.mybir import AluOpType
+
+QP, KP = 64, 128
+NP = 6
+SET = NP * QP
+KV = 2 * KP
+UNITS = [(0, "Y"), (1, "Y"), (2, "Y"), (0, "X"), (1, "X"), (2, "X"),
+         (3, "Y"), (3, "X"), (4, "Y"), (4, "X"), (5, "X"), (5, "Y")]
+NU = len(UNITS)
+NBANK = 4
+
+SCRATCH = {
+    "qsrc": ("sbuf", [128, SET], "bfloat16"),
+    "ksrc": ("sbuf", [128, NP * KP], "bfloat16"),
+    "vsrc": ("sbuf", [128, NP * KP], "bfloat16"),
+    "stage": ("sbuf", [128, (NP - 1) * KV], "bfloat16"),
+    "kvland": ("sbuf", [128, (NP - 1) * KV], "bfloat16"),
+    "qall": ("sbuf", [128, 2 * SET], "bfloat16"),
+    "zeros": ("sbuf", [128, SET], "float32"),
+    "sb": ("sbuf", [128, NU * SET], "bfloat16"),
+    "xsend": ("sbuf", [128, SET], "bfloat16"),
+    "xland": ("sbuf", [128, SET], "bfloat16"),
+    "ysend": ("sbuf", [128, SET], "bfloat16"),
+    "yland": ("sbuf", [128, SET], "bfloat16"),
+    "accx": ("psum", [128, 512], "float32"),
+    "accy": ("psum", [128, 512], "float32"),
+    "ps0": ("psum", [128, 512], "float32"),
+    "ps1": ("psum", [128, 512], "float32"),
+    "ps2": ("psum", [128, 512], "float32"),
+    "ps3": ("psum", [128, 512], "float32"),
+}
+SEMAPHORES = (["ldq", "ldk", "ldv", "z", "q0", "qarr", "qx", "odx", "ody", "xdone", "ex", "ya", "yb", "y0", "yarr", "st", "sent"]
+              + ["stg%d" % s for s in range(1, NP)] + ["kv%d" % s for s in range(1, NP)]
+              + ["sd%d" % n for n in range(NU)] + ["rd%d" % n for n in range(NU)])
+
+
+def _engines(mask):
+    return [i for i in range(mask.bit_length()) if (mask >> i) & 1]
+
+
+def _submask(engines):
+    m = 0
+    for e in engines:
+        m |= 1 << e
+    return m
+
+
+def _cols(i, w):
+    return slice(i * w, (i + 1) * w)
+
+
+def rank_program(g, core, T, topo):
+    if T.rank_of(core) is None:
+        return
+    S = T.sem
+    cores = list(T.cores)
+    plane_a = [c for c in cores if c == cores[0] or topo.same_plane(cores[0], c)]
+    plane_b = [[m for m in cores if topo.mates(a, m)][0] for a in plane_a]
+    P, M = (plane_a, plane_b) if core in plane_a else (plane_b, plane_a)
+    p = P.index(core)
+    mate = M[p]
+    head = p
+    sent = [0]
+
+    def write(dst_core, out_ap, in_ap, sem):
+        rid, pid = topo.addr(dst_core, core)
+        mask = topo.mask(core, dst_core)
+        g.remote_dma(out_ap=out_ap, in_ap=in_ap, remote_sem=sem, local_sem=S.sent, pid=pid, routing_id=rid,
+                     dma_engine_mask=mask)
+        sent[0] += len(_engines(mask))
+
+    def write_four(items, sem):
+        trs = []
+        for i, (dst_core, out_ap, in_ap) in enumerate(items):
+            rid, pid = topo.addr(dst_core, core)
+            eng = _engines(topo.mask(core, dst_core))
+            n = len(eng) // len(items)
+            trs.append(RemoteDMATransfer(dst_ids=[DstId(rid=rid, pnc=pid)], dma_engine_mask=_submask(eng[i * n:(i + 1) * n]),
+                                         remote_sem=sem, src=in_ap, dst=out_ap))
+            sent[0] += n
+        g.remote_dma_fused(trs, local_sem=S.sent)
+
+    def thin_count():
+        eng = len(_engines(topo.mask(core, P[(p + 1) % NP])))
+        return 4 * (eng // 4) + eng
+
+    off = len(_engines(topo.mask(core, P[(p + 1) % NP])))
+    off_mate = len(_engines(topo.mask(core, mate)))
+
+    g.sync.dma_start(T.qsrc[:, :], T.q[:, :]).then_inc(S.ldq, 16)
+    g.scalar.dma_start(T.ksrc[:, :], T.k[:, :]).then_inc(S.ldk, 16)
+    g.sync.dma_start(T.vsrc[:, :], T.v[:, :]).then_inc(S.ldv, 16)
+
+    g.wait_ge(S.ldq, 16)
+    write_four([(P[(p + s) % NP], T.qall[:, _cols(NP - s, QP)], T.qsrc[:, _cols((p + s) % NP, QP)]) for s in (1, 2, 3, 4)], S.qarr)
+    write(P[(p + 5) % NP], T.qall[:, _cols(NP - 5, QP)], T.qsrc[:, _cols((p + 5) % NP, QP)], S.qarr)
+
+    def send_kv(s):
+        g.wait_ge(S["stg%d" % s], 2)
+        write(P[(p + s) % NP], T.kvland[:, _cols(s - 1, KV)], T.stage[:, _cols(s - 1, KV)], S["kv%d" % s])
+
+    send_kv(1)
+    send_kv(2)
+    g.wait_ge(S.qarr, thin_count())
+    g.wait_ge(S.q0, 1)
+    write(mate, T.qall[:, SET:2 * SET], T.qall[:, 0:SET], S.qx)
+    send_kv(3)
+    send_kv(4)
+    send_kv(5)
+    g.wait_ge(S.xdone, 1)
+    write(mate, T.xland[:, :], T.xsend[:, :], S.ex)
+    g.wait_ge(S.ya, 1)
+    write_four([(P[(p + s) % NP], T.yland[:, _cols(head, QP)], T.ysend[:, _cols(s, QP)]) for s in (1, 2, 3, 4)], S.yarr)
+    g.wait_ge(S.yb, 1)
+    write(P[(p + 5) % NP], T.yland[:, _cols(head, QP)], T.ysend[:, _cols(5, QP)], S.yarr)
+    g.wait_ge(S.sent, sent[0])
+
+    pe = g.tensor
+    banks = [T.ps0, T.ps1, T.ps2, T.ps3]
+    waited = {}
+
+    def pe_wait(name, val):
+        if name not in waited:
+            waited[name] = True
+            pe.wait_ge(S[name], val)
+
+    def k_of(j):
+        return T.ksrc[:, _cols(head, KP)] if j == 0 else T.kvland[:, (j - 1) * KV:(j - 1) * KV + KP]
+
+    def v_of(j):
+        return T.vsrc[:, _cols(head, KP)] if j == 0 else T.kvland[:, (j - 1) * KV + KP:j * KV]
+
+    def mm_s(n):
+        j, qs = UNITS[n]
+        if qs == "Y":
+            pe_wait("qarr", thin_count())
+            pe_wait("q0", 1)
+        else:
+            pe_wait("qx", off_mate)
+        if j == 0:
+            pe_wait("ldk", 16)
+        else:
+            pe_wait("kv%d" % j, off)
+        rhs = T.qall[:, 0:SET] if qs == "Y" else T.qall[:, SET:2 * SET]
+        pe.matmul(banks[n % NBANK][:, 0:SET], k_of(j), rhs, True, True).then_inc(S["sd%d" % n], 1)
+
+    def mm_o(n):
+        j, qs = UNITS[n]
+        if j == 0:
+            pe_wait("ldv", 16)
+        pe.wait_ge(S["rd%d" % n], 1)
+        acc = T.accy if qs == "Y" else T.accx
+        ins = pe.matmul(acc[:, 0:SET], v_of(j), T.sb[:, _cols(n, SET)], j == 0, j == NP - 1)
+        if j == NP - 1:
+            ins.then_inc(S.ody if qs == "Y" else S.odx, 1)
+
+    mm_s(0)
+    for n in range(NU - 2):
+        mm_s(n + 1)
+        mm_o(n)
+    mm_o(NU - 2)
+    mm_s(NU - 1)
+    mm_o(NU - 1)
+
+    ve = g.vector
+    ve.memset(T.zeros[:, :], 0.0).then_inc(S.z, 1)
+    ve.wait_ge(S.ldq, 16)
+    ve.tensor_copy(T.qall[:, 0:QP], T.qsrc[:, _cols(head, QP)]).then_inc(S.q0, 1)
+    ve.wait_ge(S.ldk, 16)
+    ve.wait_ge(S.ldv, 16)
+    for s in range(1, NP):
+        hd = (p + s) % NP
+        ve.tensor_copy(T.stage[:, (s - 1) * KV:(s - 1) * KV + KP], T.ksrc[:, _cols(hd, KP)]).then_inc(S["stg%d" % s], 1)
+        ve.tensor_copy(T.stage[:, (s - 1) * KV + KP:s * KV], T.vsrc[:, _cols(hd, KP)]).then_inc(S["stg%d" % s], 1)
+    ve.wait_ge(S.z, 1)
+    for n in range(NU):
+        ve.wait_ge(S["sd%d" % n], 1)
+        ve.tensor_tensor(T.sb[:, _cols(n, SET)], banks[n % NBANK][:, 0:SET], T.zeros[:, :], AluOpType.max).then_inc(S["rd%d" % n], 1)
+        if n == NU - 2:
+            ve.wait_ge(S.odx, 1)
+            ve.tensor_copy(T.xsend[:, :], T.accx[:, 0:SET]).then_inc(S.xdone, 1)
+    ve.wait_ge(S.ody, 1)
+    ve.wait_ge(S.ex, off_mate)
+    ve.tensor_tensor(T.ysend[:, QP:5 * QP], T.accy[:, QP:5 * QP], T.xland[:, QP:5 * QP], AluOpType.add).then_inc(S.ya, 1)
+    ve.tensor_tensor(T.ysend[:, 5 * QP:SET], T.accy[:, 5 * QP:SET], T.xland[:, 5 * QP:SET], AluOpType.add).then_inc(S.yb, 1)
+    ve.tensor_tensor(T.yland[:, _cols(head, QP)], T.accy[:, 0:QP], T.xland[:, 0:QP], AluOpType.add).then_inc(S.y0, 1)
+
+    g.sync.wait_ge(S.yarr, thin_count())
+    g.sync.wait_ge(S.y0, 1)
+    g.sync.dma_start(T.y[:, :], T.yland[:, :]).then_inc(S.st, 16)
+    g.sync.wait_ge(S.st, 16)

@@ -5,9 +5,11 @@ QP, KP = 64, 128
 NP = 6
 SET = NP * QP
 KV = 2 * KP
-UNITS = [(0, "Y"), (1, "Y"), (2, "Y"), (0, "X"), (1, "X"), (2, "X"),
-         (3, "Y"), (3, "X"), (4, "Y"), (4, "X"), (5, "X"), (5, "Y")]
+UNITS = [(0, "Y"), (1, "Y"), (0, "X"), (1, "X"), (2, "X"), (3, "X"),
+         (4, "X"), (5, "X"), (2, "Y"), (3, "Y"), (4, "Y"), (5, "Y")]
 NU = len(UNITS)
+LASTX = UNITS.index((NP - 1, "X"))
+LASTK = NP - 1
 NBANK = 4
 
 SCRATCH = {
@@ -30,7 +32,7 @@ SCRATCH = {
     "ps2": ("psum", [128, 512], "float32"),
     "ps3": ("psum", [128, 512], "float32"),
 }
-SEMAPHORES = (["ldq", "ldk", "ldv", "z", "q0", "qarr", "qx", "odx", "ody", "xdone", "ex", "ya", "yb", "y0", "yarr", "st", "sent"]
+SEMAPHORES = (["ldq", "ldk", "ldv", "z", "q0", "qarr", "qx", "odx", "ody", "xdone", "ex", "ya", "yb", "y0", "yarr", "st", "sent", "vlast"]
               + ["stg%d" % s for s in range(1, NP)] + ["kv%d" % s for s in range(1, NP)]
               + ["sd%d" % n for n in range(NU)] + ["rd%d" % n for n in range(NU)])
 
@@ -101,13 +103,17 @@ def rank_program(g, core, T, topo):
         write(P[(p + s) % NP], T.kvland[:, _cols(s - 1, KV)], T.stage[:, _cols(s - 1, KV)], S["kv%d" % s])
 
     send_kv(1)
-    send_kv(2)
     g.wait_ge(S.qarr, thin_count())
     g.wait_ge(S.q0, 1)
     write(mate, T.qall[:, SET:2 * SET], T.qall[:, 0:SET], S.qx)
+    send_kv(2)
     send_kv(3)
     send_kv(4)
-    send_kv(5)
+    g.wait_ge(S["stg%d" % LASTK], 2)
+    kcols = slice((LASTK - 1) * KV, (LASTK - 1) * KV + KP)
+    vcols = slice((LASTK - 1) * KV + KP, LASTK * KV)
+    write(P[(p + LASTK) % NP], T.kvland[:, kcols], T.stage[:, kcols], S["kv%d" % LASTK])
+    write(P[(p + LASTK) % NP], T.kvland[:, vcols], T.stage[:, vcols], S.vlast)
     g.wait_ge(S.xdone, 1)
     write(mate, T.xland[:, :], T.xsend[:, :], S.ex)
     g.wait_ge(S.ya, 1)
@@ -149,6 +155,8 @@ def rank_program(g, core, T, topo):
         j, qs = UNITS[n]
         if j == 0:
             pe_wait("ldv", 16)
+        if j == LASTK:
+            pe_wait("vlast", off)
         pe.wait_ge(S["rd%d" % n], 1)
         acc = T.accy if qs == "Y" else T.accx
         ins = pe.matmul(acc[:, 0:SET], v_of(j), T.sb[:, _cols(n, SET)], j == 0, j == NP - 1)
@@ -156,12 +164,13 @@ def rank_program(g, core, T, topo):
             ins.then_inc(S.ody if qs == "Y" else S.odx, 1)
 
     mm_s(0)
-    for n in range(NU - 2):
-        mm_s(n + 1)
+    ahead = 1
+    for n in range(NU):
+        want = n + 3 if n >= LASTX else n + 2
+        while ahead < min(want, NU):
+            mm_s(ahead)
+            ahead += 1
         mm_o(n)
-    mm_o(NU - 2)
-    mm_s(NU - 1)
-    mm_o(NU - 1)
 
     ve = g.vector
     ve.memset(T.zeros[:, :], 0.0).then_inc(S.z, 1)
@@ -177,7 +186,7 @@ def rank_program(g, core, T, topo):
     for n in range(NU):
         ve.wait_ge(S["sd%d" % n], 1)
         ve.tensor_tensor(T.sb[:, _cols(n, SET)], banks[n % NBANK][:, 0:SET], T.zeros[:, :], AluOpType.max).then_inc(S["rd%d" % n], 1)
-        if n == NU - 2:
+        if n == LASTX + 1:
             ve.wait_ge(S.odx, 1)
             ve.tensor_copy(T.xsend[:, :], T.accx[:, 0:SET]).then_inc(S.xdone, 1)
     ve.wait_ge(S.ody, 1)

@@ -5,10 +5,6 @@ QP, KP = 64, 128
 NP = 6
 SET = NP * QP
 KV = 2 * KP
-UNITS = [(0, "Y"), (1, "Y"), (0, "X"), (1, "X"), (2, "X"), (3, "X"),
-         (4, "X"), (5, "X"), (2, "Y"), (3, "Y"), (4, "Y"), (5, "Y")]
-NU = len(UNITS)
-LASTX = UNITS.index((NP - 1, "X"))
 LASTK = NP - 1
 NBANK = 4
 
@@ -16,25 +12,25 @@ SCRATCH = {
     "qsrc": ("sbuf", [128, SET], "bfloat16"),
     "ksrc": ("sbuf", [128, NP * KP], "bfloat16"),
     "vsrc": ("sbuf", [128, NP * KP], "bfloat16"),
-    "stage": ("sbuf", [128, (NP - 1) * KV], "bfloat16"),
-    "kvland": ("sbuf", [128, (NP - 1) * KV], "bfloat16"),
-    "qall": ("sbuf", [128, 2 * SET], "bfloat16"),
+    "stage": ("sbuf", [128, NP * KV], "bfloat16"),
+    "kvland": ("sbuf", [128, NP * KV], "bfloat16"),
+    "qall": ("sbuf", [128, SET], "bfloat16"),
     "zeros": ("sbuf", [128, SET], "float32"),
-    "sb": ("sbuf", [128, NU * SET], "bfloat16"),
-    "xsend": ("sbuf", [128, SET], "bfloat16"),
-    "xland": ("sbuf", [128, SET], "bfloat16"),
+    "sb": ("sbuf", [128, NP * SET], "bfloat16"),
     "ysend": ("sbuf", [128, SET], "bfloat16"),
-    "yland": ("sbuf", [128, SET], "bfloat16"),
-    "accx": ("psum", [128, 512], "float32"),
-    "accy": ("psum", [128, 512], "float32"),
+    "ya": ("sbuf", [128, SET], "bfloat16"),
+    "yb": ("sbuf", [128, SET], "bfloat16"),
+    "yout": ("sbuf", [128, SET], "bfloat16"),
+    "acc": ("psum", [128, 512], "float32"),
     "ps0": ("psum", [128, 512], "float32"),
     "ps1": ("psum", [128, 512], "float32"),
     "ps2": ("psum", [128, 512], "float32"),
     "ps3": ("psum", [128, 512], "float32"),
 }
-SEMAPHORES = (["ldq", "ldk", "ldv", "z", "q0", "qarr", "qx", "odx", "ody", "xdone", "ex", "ya", "yb", "y0", "yarr", "st", "sent", "vlast"]
-              + ["stg%d" % s for s in range(1, NP)] + ["kv%d" % s for s in range(1, NP)]
-              + ["sd%d" % n for n in range(NU)] + ["rd%d" % n for n in range(NU)])
+SEMAPHORES = (["ldq", "ldk", "ldv", "z", "q0", "qarr", "qx", "od", "c1", "c2", "y0", "arra1", "arra2", "arrb1", "arrb2",
+               "yf1", "yf2", "st1", "st2", "sent", "klast", "vlast"]
+              + ["stg%d" % s for s in range(NP)] + ["kv%d" % s for s in range(LASTK)]
+              + ["sd%d" % n for n in range(NP)] + ["rd%d" % n for n in range(NP)])
 
 
 def _engines(mask):
@@ -52,27 +48,63 @@ def _cols(i, w):
     return slice(i * w, (i + 1) * w)
 
 
+def _runs(heads):
+    out = []
+    for h in sorted(heads):
+        if out and out[-1][1] == h:
+            out[-1][1] = h + 1
+        else:
+            out.append([h, h + 1])
+    return [slice(a * QP, b * QP) for a, b in out]
+
+
+def _sibling(r, m, T, topo):
+    world = (max(topo.host(c) for c in T.cores) + 1) * topo.CORES_PER_HOST
+    return [c for c in range(world)
+            if c != r and topo.host(c) == topo.host(r) and topo.chip(c) == topo.chip(r) and topo.die(c) == topo.die(r)
+            and T.rank_of(c) is None and topo.may_write(c, m)][0]
+
+
 def rank_program(g, core, T, topo):
-    if T.rank_of(core) is None:
-        return
     S = T.sem
     cores = list(T.cores)
     plane_a = [c for c in cores if c == cores[0] or topo.same_plane(cores[0], c)]
     plane_b = [[m for m in cores if topo.mates(a, m)][0] for a in plane_a]
-    P, M = (plane_a, plane_b) if core in plane_a else (plane_b, plane_a)
-    p = P.index(core)
-    mate = M[p]
+    sib_a = [_sibling(a, b, T, topo) for a, b in zip(plane_a, plane_b)]
+    sib_b = [_sibling(b, a, T, topo) for a, b in zip(plane_a, plane_b)]
+    if core in plane_a:
+        is_rank, P, M, GP, GM, p = True, plane_a, plane_b, sib_a, sib_b, plane_a.index(core)
+    elif core in plane_b:
+        is_rank, P, M, GP, GM, p = True, plane_b, plane_a, sib_b, sib_a, plane_b.index(core)
+    elif core in sib_a:
+        is_rank, P, M, GP, GM, p = False, plane_a, plane_b, sib_a, sib_b, sib_a.index(core)
+    elif core in sib_b:
+        is_rank, P, M, GP, GM, p = False, plane_b, plane_a, sib_b, sib_a, sib_b.index(core)
+    else:
+        return
     head = p
+    R, G = P[p], GP[p]
     sent = [0]
 
-    def write(dst_core, out_ap, in_ap, sem):
+    far = topo.mask(R, P[(p + 1) % NP])
+    off = len(_engines(far))
+    near_only = topo.mask(R, G) & ~far
+    own_mask = near_only if near_only else topo.mask(R, G)
+    n_own = len(_engines(own_mask))
+    pass_mask = topo.mask(G, R) & topo.mask(G, M[p])
+    n_pass = len(_engines(pass_mask))
+    off_mate = len(_engines(topo.mask(R, GM[p])))
+    thin5 = 4 * (off // 4) + off
+
+    def write(dst_core, out_ap, in_ap, sem, mask=None):
         rid, pid = topo.addr(dst_core, core)
-        mask = topo.mask(core, dst_core)
+        if mask is None:
+            mask = topo.mask(core, dst_core)
         g.remote_dma(out_ap=out_ap, in_ap=in_ap, remote_sem=sem, local_sem=S.sent, pid=pid, routing_id=rid,
                      dma_engine_mask=mask)
         sent[0] += len(_engines(mask))
 
-    def write_four(items, sem):
+    def write_side_by_side(items, sem):
         trs = []
         for i, (dst_core, out_ap, in_ap) in enumerate(items):
             rid, pid = topo.addr(dst_core, core)
@@ -83,44 +115,52 @@ def rank_program(g, core, T, topo):
             sent[0] += n
         g.remote_dma_fused(trs, local_sem=S.sent)
 
-    def thin_count():
-        eng = len(_engines(topo.mask(core, P[(p + 1) % NP])))
-        return 4 * (eng // 4) + eng
+    kcols = slice(LASTK * KV, LASTK * KV + KP)
+    vcols = slice(LASTK * KV + KP, NP * KV)
 
-    off = len(_engines(topo.mask(core, P[(p + 1) % NP])))
-    off_mate = len(_engines(topo.mask(core, mate)))
+    if is_rank:
+        g.sync.dma_start(T.qsrc[:, :], T.q[:, :]).then_inc(S.ldq, 16)
+        g.scalar.dma_start(T.ksrc[:, :], T.k[:, :]).then_inc(S.ldk, 16)
+        g.sync.dma_start(T.vsrc[:, :], T.v[:, :]).then_inc(S.ldv, 16)
 
-    g.sync.dma_start(T.qsrc[:, :], T.q[:, :]).then_inc(S.ldq, 16)
-    g.scalar.dma_start(T.ksrc[:, :], T.k[:, :]).then_inc(S.ldk, 16)
-    g.sync.dma_start(T.vsrc[:, :], T.v[:, :]).then_inc(S.ldv, 16)
+        g.wait_ge(S.ldq, 16)
+        write_side_by_side([(P[(p + s) % NP], T.qall[:, _cols(NP - s, QP)], T.qsrc[:, _cols((p + s) % NP, QP)])
+                            for s in (1, 2, 3, 4)], S.qarr)
+        write(P[(p + 5) % NP], T.qall[:, _cols(NP - 5, QP)], T.qsrc[:, _cols((p + 5) % NP, QP)], S.qarr)
 
-    g.wait_ge(S.ldq, 16)
-    write_four([(P[(p + s) % NP], T.qall[:, _cols(NP - s, QP)], T.qsrc[:, _cols((p + s) % NP, QP)]) for s in (1, 2, 3, 4)], S.qarr)
-    write(P[(p + 5) % NP], T.qall[:, _cols(NP - 5, QP)], T.qsrc[:, _cols((p + 5) % NP, QP)], S.qarr)
+        def send_kv(s):
+            g.wait_ge(S["stg%d" % s], 2)
+            write(GP[(p + s) % NP], T.kvland[:, _cols(s, KV)], T.stage[:, _cols(s, KV)], S["kv%d" % s])
 
-    def send_kv(s):
-        g.wait_ge(S["stg%d" % s], 2)
-        write(P[(p + s) % NP], T.kvland[:, _cols(s - 1, KV)], T.stage[:, _cols(s - 1, KV)], S["kv%d" % s])
-
-    send_kv(1)
-    g.wait_ge(S.qarr, thin_count())
-    g.wait_ge(S.q0, 1)
-    write(mate, T.qall[:, SET:2 * SET], T.qall[:, 0:SET], S.qx)
-    send_kv(2)
-    send_kv(3)
-    send_kv(4)
-    g.wait_ge(S["stg%d" % LASTK], 2)
-    kcols = slice((LASTK - 1) * KV, (LASTK - 1) * KV + KP)
-    vcols = slice((LASTK - 1) * KV + KP, LASTK * KV)
-    write(P[(p + LASTK) % NP], T.kvland[:, kcols], T.stage[:, kcols], S["kv%d" % LASTK])
-    write(P[(p + LASTK) % NP], T.kvland[:, vcols], T.stage[:, vcols], S.vlast)
-    g.wait_ge(S.xdone, 1)
-    write(mate, T.xland[:, :], T.xsend[:, :], S.ex)
-    g.wait_ge(S.ya, 1)
-    write_four([(P[(p + s) % NP], T.yland[:, _cols(head, QP)], T.ysend[:, _cols(s, QP)]) for s in (1, 2, 3, 4)], S.yarr)
-    g.wait_ge(S.yb, 1)
-    write(P[(p + 5) % NP], T.yland[:, _cols(head, QP)], T.ysend[:, _cols(5, QP)], S.yarr)
-    g.wait_ge(S.sent, sent[0])
+        send_kv(1)
+        g.wait_ge(S.stg0, 2)
+        write(G, T.kvland[:, _cols(0, KV)], T.stage[:, _cols(0, KV)], S.kv0, own_mask)
+        g.wait_ge(S.qarr, thin5)
+        g.wait_ge(S.q0, 1)
+        write(GM[p], T.qall[:, :], T.qall[:, :], S.qx)
+        send_kv(2)
+        send_kv(3)
+        send_kv(4)
+        g.wait_ge(S["stg%d" % LASTK], 2)
+        dg, dr = GP[(p + LASTK) % NP], P[(p + LASTK) % NP]
+        write(dg, T.kvland[:, kcols], T.stage[:, kcols], S.klast)
+        write(dr, T.kvland[:, kcols], T.stage[:, kcols], S.klast)
+        write(dg, T.kvland[:, vcols], T.stage[:, vcols], S.vlast)
+        write(dr, T.kvland[:, vcols], T.stage[:, vcols], S.vlast)
+        g.wait_ge(S.c1, 1)
+        write_side_by_side([(P[(p + s) % NP], T.ya[:, _cols(head, QP)], T.ysend[:, _cols(s, QP)]) for s in (1, 2, 3, 4)], S.arra1)
+        g.wait_ge(S.c2, 1)
+        write(P[(p + 5) % NP], T.ya[:, _cols(head, QP)], T.ysend[:, _cols(5, QP)], S.arra2)
+        g.wait_ge(S.sent, sent[0])
+    else:
+        for s in range(1, LASTK):
+            g.wait_ge(S["kv%d" % s], off)
+            write(R, T.kvland[:, _cols(s, KV)], T.kvland[:, _cols(s, KV)], S["kv%d" % s], pass_mask)
+        g.wait_ge(S.c1, 1)
+        write_side_by_side([(M[(p + t) % NP], T.yb[:, _cols(head, QP)], T.ysend[:, _cols(t, QP)]) for t in (0, 1, 2, 3)], S.arrb1)
+        g.wait_ge(S.c2, 1)
+        write_side_by_side([(M[(p + t) % NP], T.yb[:, _cols(head, QP)], T.ysend[:, _cols(t, QP)]) for t in (4, 5)], S.arrb2)
+        g.wait_ge(S.sent, sent[0])
 
     pe = g.tensor
     banks = [T.ps0, T.ps1, T.ps2, T.ps3]
@@ -131,71 +171,82 @@ def rank_program(g, core, T, topo):
             waited[name] = True
             pe.wait_ge(S[name], val)
 
-    def k_of(j):
-        return T.ksrc[:, _cols(head, KP)] if j == 0 else T.kvland[:, (j - 1) * KV:(j - 1) * KV + KP]
+    def kv_of(j):
+        buf = T.stage if (is_rank and j == 0) else T.kvland
+        return buf[:, j * KV:j * KV + KP], buf[:, j * KV + KP:(j + 1) * KV]
 
-    def v_of(j):
-        return T.vsrc[:, _cols(head, KP)] if j == 0 else T.kvland[:, (j - 1) * KV + KP:j * KV]
+    def wait_block(j, part):
+        if j == LASTK:
+            pe_wait("klast" if part == "k" else "vlast", off)
+        elif j == 0:
+            if is_rank:
+                pe_wait("stg0", 2)
+            else:
+                pe_wait("kv0", n_own)
+        else:
+            pe_wait("kv%d" % j, n_pass if is_rank else off)
 
-    def mm_s(n):
-        j, qs = UNITS[n]
-        if qs == "Y":
-            pe_wait("qarr", thin_count())
+    def mm_s(j):
+        if is_rank:
+            pe_wait("qarr", thin5)
             pe_wait("q0", 1)
         else:
             pe_wait("qx", off_mate)
-        if j == 0:
-            pe_wait("ldk", 16)
-        else:
-            pe_wait("kv%d" % j, off)
-        rhs = T.qall[:, 0:SET] if qs == "Y" else T.qall[:, SET:2 * SET]
-        pe.matmul(banks[n % NBANK][:, 0:SET], k_of(j), rhs, True, True).then_inc(S["sd%d" % n], 1)
+        wait_block(j, "k")
+        pe.matmul(banks[j % NBANK][:, 0:SET], kv_of(j)[0], T.qall[:, :], True, True).then_inc(S["sd%d" % j], 1)
 
-    def mm_o(n):
-        j, qs = UNITS[n]
-        if j == 0:
-            pe_wait("ldv", 16)
-        if j == LASTK:
-            pe_wait("vlast", off)
-        pe.wait_ge(S["rd%d" % n], 1)
-        acc = T.accy if qs == "Y" else T.accx
-        ins = pe.matmul(acc[:, 0:SET], v_of(j), T.sb[:, _cols(n, SET)], j == 0, j == NP - 1)
+    def mm_o(j):
+        wait_block(j, "v")
+        pe.wait_ge(S["rd%d" % j], 1)
+        ins = pe.matmul(T.acc[:, 0:SET], kv_of(j)[1], T.sb[:, _cols(j, SET)], j == 0, j == NP - 1)
         if j == NP - 1:
-            ins.then_inc(S.ody if qs == "Y" else S.odx, 1)
+            ins.then_inc(S.od, 1)
 
     mm_s(0)
-    ahead = 1
-    for n in range(NU):
-        want = n + 3 if n >= LASTX else n + 2
-        while ahead < min(want, NU):
-            mm_s(ahead)
-            ahead += 1
-        mm_o(n)
+    for j in range(NP):
+        if j + 1 < NP:
+            mm_s(j + 1)
+        mm_o(j)
 
     ve = g.vector
     ve.memset(T.zeros[:, :], 0.0).then_inc(S.z, 1)
-    ve.wait_ge(S.ldq, 16)
-    ve.tensor_copy(T.qall[:, 0:QP], T.qsrc[:, _cols(head, QP)]).then_inc(S.q0, 1)
-    ve.wait_ge(S.ldk, 16)
-    ve.wait_ge(S.ldv, 16)
-    for s in range(1, NP):
-        hd = (p + s) % NP
-        ve.tensor_copy(T.stage[:, (s - 1) * KV:(s - 1) * KV + KP], T.ksrc[:, _cols(hd, KP)]).then_inc(S["stg%d" % s], 1)
-        ve.tensor_copy(T.stage[:, (s - 1) * KV + KP:s * KV], T.vsrc[:, _cols(hd, KP)]).then_inc(S["stg%d" % s], 1)
+    if is_rank:
+        ve.wait_ge(S.ldq, 16)
+        ve.tensor_copy(T.qall[:, 0:QP], T.qsrc[:, _cols(head, QP)]).then_inc(S.q0, 1)
+        ve.wait_ge(S.ldk, 16)
+        ve.wait_ge(S.ldv, 16)
+        for s in (1, 0, 2, 3, 4, 5):
+            hd = (p + s) % NP
+            ve.tensor_copy(T.stage[:, s * KV:s * KV + KP], T.ksrc[:, _cols(hd, KP)]).then_inc(S["stg%d" % s], 1)
+            ve.tensor_copy(T.stage[:, s * KV + KP:(s + 1) * KV], T.vsrc[:, _cols(hd, KP)]).then_inc(S["stg%d" % s], 1)
     ve.wait_ge(S.z, 1)
-    for n in range(NU):
-        ve.wait_ge(S["sd%d" % n], 1)
-        ve.tensor_tensor(T.sb[:, _cols(n, SET)], banks[n % NBANK][:, 0:SET], T.zeros[:, :], AluOpType.max).then_inc(S["rd%d" % n], 1)
-        if n == LASTX + 1:
-            ve.wait_ge(S.odx, 1)
-            ve.tensor_copy(T.xsend[:, :], T.accx[:, 0:SET]).then_inc(S.xdone, 1)
-    ve.wait_ge(S.ody, 1)
-    ve.wait_ge(S.ex, off_mate)
-    ve.tensor_tensor(T.ysend[:, QP:5 * QP], T.accy[:, QP:5 * QP], T.xland[:, QP:5 * QP], AluOpType.add).then_inc(S.ya, 1)
-    ve.tensor_tensor(T.ysend[:, 5 * QP:SET], T.accy[:, 5 * QP:SET], T.xland[:, 5 * QP:SET], AluOpType.add).then_inc(S.yb, 1)
-    ve.tensor_tensor(T.yland[:, _cols(head, QP)], T.accy[:, 0:QP], T.xland[:, 0:QP], AluOpType.add).then_inc(S.y0, 1)
-
-    g.sync.wait_ge(S.yarr, thin_count())
-    g.sync.wait_ge(S.y0, 1)
-    g.sync.dma_start(T.y[:, :], T.yland[:, :]).then_inc(S.st, 16)
-    g.sync.wait_ge(S.st, 16)
+    for j in range(NP):
+        ve.wait_ge(S["sd%d" % j], 1)
+        ve.tensor_tensor(T.sb[:, _cols(j, SET)], banks[j % NBANK][:, 0:SET], T.zeros[:, :], AluOpType.max).then_inc(S["rd%d" % j], 1)
+    ve.wait_ge(S.od, 1)
+    if is_rank:
+        ve.tensor_copy(T.ysend[:, QP:5 * QP], T.acc[:, QP:5 * QP]).then_inc(S.c1, 1)
+        ve.tensor_copy(T.ysend[:, 5 * QP:SET], T.acc[:, 5 * QP:SET]).then_inc(S.c2, 1)
+        ve.tensor_copy(T.ya[:, _cols(head, QP)], T.acc[:, 0:QP]).then_inc(S.y0, 1)
+        early = _runs([(p - d) % NP for d in (0, 1, 2, 3)])
+        late = _runs([(p - d) % NP for d in (4, 5)])
+        ve.wait_ge(S.y0, 1)
+        ve.wait_ge(S.arra1, 4 * (off // 4))
+        ve.wait_ge(S.arrb1, 4 * (off // 4))
+        for c in early:
+            ve.tensor_tensor(T.yout[:, c], T.ya[:, c], T.yb[:, c], AluOpType.add).then_inc(S.yf1, 1)
+        ve.wait_ge(S.arra2, off)
+        ve.wait_ge(S.arrb2, 2 * (off // 2))
+        for c in late:
+            ve.tensor_tensor(T.yout[:, c], T.ya[:, c], T.yb[:, c], AluOpType.add).then_inc(S.yf2, 1)
+        g.scalar.wait_ge(S.yf1, len(early))
+        for c in early:
+            g.scalar.dma_start(T.y[:, c], T.yout[:, c]).then_inc(S.st1, 16)
+        g.scalar.wait_ge(S.st1, 16 * len(early))
+        g.sync.wait_ge(S.yf2, len(late))
+        for c in late:
+            g.sync.dma_start(T.y[:, c], T.yout[:, c]).then_inc(S.st2, 16)
+        g.sync.wait_ge(S.st2, 16 * len(late))
+    else:
+        ve.tensor_copy(T.ysend[:, 0:4 * QP], T.acc[:, 0:4 * QP]).then_inc(S.c1, 1)
+        ve.tensor_copy(T.ysend[:, 4 * QP:SET], T.acc[:, 4 * QP:SET]).then_inc(S.c2, 1)

from concourse.bass import DstId, RemoteDMATransfer
from concourse.mybir import AluOpType

QP, KP = 64, 128
NP = 6
SET = NP * QP
KV = 2 * KP
LASTK = NP - 1
NBANK = 4

SCRATCH = {
    "qsrc": ("sbuf", [128, SET], "bfloat16"),
    "ksrc": ("sbuf", [128, NP * KP], "bfloat16"),
    "vsrc": ("sbuf", [128, NP * KP], "bfloat16"),
    "stage": ("sbuf", [128, NP * KV], "bfloat16"),
    "kvland": ("sbuf", [128, NP * KV], "bfloat16"),
    "qall": ("sbuf", [128, SET], "bfloat16"),
    "zeros": ("sbuf", [128, SET], "float32"),
    "sb": ("sbuf", [128, NP * SET], "bfloat16"),
    "ysend": ("sbuf", [128, SET], "bfloat16"),
    "ya": ("sbuf", [128, SET], "bfloat16"),
    "yb": ("sbuf", [128, SET], "bfloat16"),
    "yout": ("sbuf", [128, SET], "bfloat16"),
    "acc": ("psum", [128, 512], "float32"),
    "ps0": ("psum", [128, 512], "float32"),
    "ps1": ("psum", [128, 512], "float32"),
    "ps2": ("psum", [128, 512], "float32"),
    "ps3": ("psum", [128, 512], "float32"),
}
SEMAPHORES = (["ldq", "ldk", "ldv", "z", "q0", "qarr", "qx", "od", "c1", "c2", "y0", "arra1", "arra2", "arrb1", "arrb2",
               "yf1", "yf2", "st1", "st2", "sent", "klast", "vlast"]
              + ["stg%d" % s for s in range(NP)] + ["kv%d" % s for s in range(LASTK)]
              + ["sd%d" % n for n in range(NP)] + ["rd%d" % n for n in range(NP)])


def _engines(mask):
    return [i for i in range(mask.bit_length()) if (mask >> i) & 1]


def _submask(engines):
    m = 0
    for e in engines:
        m |= 1 << e
    return m


def _cols(i, w):
    return slice(i * w, (i + 1) * w)


def _runs(heads):
    out = []
    for h in sorted(heads):
        if out and out[-1][1] == h:
            out[-1][1] = h + 1
        else:
            out.append([h, h + 1])
    return [slice(a * QP, b * QP) for a, b in out]


def _sibling(r, m, T, topo):
    world = (max(topo.host(c) for c in T.cores) + 1) * topo.CORES_PER_HOST
    return [c for c in range(world)
            if c != r and topo.host(c) == topo.host(r) and topo.chip(c) == topo.chip(r) and topo.die(c) == topo.die(r)
            and T.rank_of(c) is None and topo.may_write(c, m)][0]


def rank_program(g, core, T, topo):
    S = T.sem
    cores = list(T.cores)
    plane_a = [c for c in cores if c == cores[0] or topo.same_plane(cores[0], c)]
    plane_b = [[m for m in cores if topo.mates(a, m)][0] for a in plane_a]
    sib_a = [_sibling(a, b, T, topo) for a, b in zip(plane_a, plane_b)]
    sib_b = [_sibling(b, a, T, topo) for a, b in zip(plane_a, plane_b)]
    if core in plane_a:
        is_rank, P, M, GP, GM, p = True, plane_a, plane_b, sib_a, sib_b, plane_a.index(core)
    elif core in plane_b:
        is_rank, P, M, GP, GM, p = True, plane_b, plane_a, sib_b, sib_a, plane_b.index(core)
    elif core in sib_a:
        is_rank, P, M, GP, GM, p = False, plane_a, plane_b, sib_a, sib_b, sib_a.index(core)
    elif core in sib_b:
        is_rank, P, M, GP, GM, p = False, plane_b, plane_a, sib_b, sib_a, sib_b.index(core)
    else:
        return
    head = p
    R, G = P[p], GP[p]
    sent = [0]

    far = topo.mask(R, P[(p + 1) % NP])
    off = len(_engines(far))
    near_only = topo.mask(R, G) & ~far
    own_mask = near_only if near_only else topo.mask(R, G)
    n_own = len(_engines(own_mask))
    pass_mask = topo.mask(G, R) & topo.mask(G, M[p])
    n_pass = len(_engines(pass_mask))
    off_mate = len(_engines(topo.mask(R, GM[p])))
    thin5 = 4 * (off // 4) + off

    def write(dst_core, out_ap, in_ap, sem, mask=None):
        rid, pid = topo.addr(dst_core, core)
        if mask is None:
            mask = topo.mask(core, dst_core)
        g.remote_dma(out_ap=out_ap, in_ap=in_ap, remote_sem=sem, local_sem=S.sent, pid=pid, routing_id=rid,
                     dma_engine_mask=mask)
        sent[0] += len(_engines(mask))

    def write_side_by_side(items, sem):
        trs = []
        for i, (dst_core, out_ap, in_ap) in enumerate(items):
            rid, pid = topo.addr(dst_core, core)
            eng = _engines(topo.mask(core, dst_core))
            n = len(eng) // len(items)
            trs.append(RemoteDMATransfer(dst_ids=[DstId(rid=rid, pnc=pid)], dma_engine_mask=_submask(eng[i * n:(i + 1) * n]),
                                         remote_sem=sem, src=in_ap, dst=out_ap))
            sent[0] += n
        g.remote_dma_fused(trs, local_sem=S.sent)

    kcols = slice(LASTK * KV, LASTK * KV + KP)
    vcols = slice(LASTK * KV + KP, NP * KV)

    if is_rank:
        g.sync.dma_start(T.qsrc[:, :], T.q[:, :]).then_inc(S.ldq, 16)
        g.scalar.dma_start(T.ksrc[:, :], T.k[:, :]).then_inc(S.ldk, 16)
        g.sync.dma_start(T.vsrc[:, :], T.v[:, :]).then_inc(S.ldv, 16)

        g.wait_ge(S.ldq, 16)
        write_side_by_side([(P[(p + s) % NP], T.qall[:, _cols(NP - s, QP)], T.qsrc[:, _cols((p + s) % NP, QP)])
                            for s in (1, 2, 3, 4)], S.qarr)
        write(P[(p + 5) % NP], T.qall[:, _cols(NP - 5, QP)], T.qsrc[:, _cols((p + 5) % NP, QP)], S.qarr)

        def send_kv(s):
            g.wait_ge(S["stg%d" % s], 2)
            write(GP[(p + s) % NP], T.kvland[:, _cols(s, KV)], T.stage[:, _cols(s, KV)], S["kv%d" % s])

        send_kv(1)
        g.wait_ge(S.stg0, 2)
        write(G, T.kvland[:, _cols(0, KV)], T.stage[:, _cols(0, KV)], S.kv0, own_mask)
        g.wait_ge(S.qarr, thin5)
        g.wait_ge(S.q0, 1)
        write(GM[p], T.qall[:, :], T.qall[:, :], S.qx)
        send_kv(2)
        send_kv(3)
        send_kv(4)
        g.wait_ge(S["stg%d" % LASTK], 2)
        dg, dr = GP[(p + LASTK) % NP], P[(p + LASTK) % NP]
        write(dg, T.kvland[:, kcols], T.stage[:, kcols], S.klast)
        write(dr, T.kvland[:, kcols], T.stage[:, kcols], S.klast)
        write(dg, T.kvland[:, vcols], T.stage[:, vcols], S.vlast)
        write(dr, T.kvland[:, vcols], T.stage[:, vcols], S.vlast)
        g.wait_ge(S.c1, 1)
        write_side_by_side([(P[(p + s) % NP], T.ya[:, _cols(head, QP)], T.ysend[:, _cols(s, QP)]) for s in (1, 2, 3, 4)], S.arra1)
        g.wait_ge(S.c2, 1)
        write(P[(p + 5) % NP], T.ya[:, _cols(head, QP)], T.ysend[:, _cols(5, QP)], S.arra2)
        g.wait_ge(S.sent, sent[0])
    else:
        for s in range(1, LASTK):
            g.wait_ge(S["kv%d" % s], off)
            write(R, T.kvland[:, _cols(s, KV)], T.kvland[:, _cols(s, KV)], S["kv%d" % s], pass_mask)
        g.wait_ge(S.c1, 1)
        write_side_by_side([(M[(p + t) % NP], T.yb[:, _cols(head, QP)], T.ysend[:, _cols(t, QP)]) for t in (0, 1, 2, 3)], S.arrb1)
        g.wait_ge(S.c2, 1)
        write_side_by_side([(M[(p + t) % NP], T.yb[:, _cols(head, QP)], T.ysend[:, _cols(t, QP)]) for t in (4, 5)], S.arrb2)
        g.wait_ge(S.sent, sent[0])

    pe = g.tensor
    banks = [T.ps0, T.ps1, T.ps2, T.ps3]
    waited = {}

    def pe_wait(name, val):
        if name not in waited:
            waited[name] = True
            pe.wait_ge(S[name], val)

    def kv_of(j):
        buf = T.stage if (is_rank and j == 0) else T.kvland
        return buf[:, j * KV:j * KV + KP], buf[:, j * KV + KP:(j + 1) * KV]

    def wait_block(j, part):
        if j == LASTK:
            pe_wait("klast" if part == "k" else "vlast", off)
        elif j == 0:
            if is_rank:
                pe_wait("stg0", 2)
            else:
                pe_wait("kv0", n_own)
        else:
            pe_wait("kv%d" % j, n_pass if is_rank else off)

    def mm_s(j):
        if is_rank:
            pe_wait("qarr", thin5)
            pe_wait("q0", 1)
        else:
            pe_wait("qx", off_mate)
        wait_block(j, "k")
        pe.matmul(banks[j % NBANK][:, 0:SET], kv_of(j)[0], T.qall[:, :], True, True).then_inc(S["sd%d" % j], 1)

    def mm_o(j):
        wait_block(j, "v")
        pe.wait_ge(S["rd%d" % j], 1)
        ins = pe.matmul(T.acc[:, 0:SET], kv_of(j)[1], T.sb[:, _cols(j, SET)], j == 0, j == NP - 1)
        if j == NP - 1:
            ins.then_inc(S.od, 1)

    mm_s(0)
    for j in range(NP):
        if j + 1 < NP:
            mm_s(j + 1)
        mm_o(j)

    ve = g.vector
    ve.memset(T.zeros[:, :], 0.0).then_inc(S.z, 1)
    if is_rank:
        ve.wait_ge(S.ldq, 16)
        ve.tensor_copy(T.qall[:, 0:QP], T.qsrc[:, _cols(head, QP)]).then_inc(S.q0, 1)
        ve.wait_ge(S.ldk, 16)
        ve.wait_ge(S.ldv, 16)
        for s in (1, 0, 2, 3, 4, 5):
            hd = (p + s) % NP
            ve.tensor_copy(T.stage[:, s * KV:s * KV + KP], T.ksrc[:, _cols(hd, KP)]).then_inc(S["stg%d" % s], 1)
            ve.tensor_copy(T.stage[:, s * KV + KP:(s + 1) * KV], T.vsrc[:, _cols(hd, KP)]).then_inc(S["stg%d" % s], 1)
    ve.wait_ge(S.z, 1)
    for j in range(NP):
        ve.wait_ge(S["sd%d" % j], 1)
        ve.tensor_tensor(T.sb[:, _cols(j, SET)], banks[j % NBANK][:, 0:SET], T.zeros[:, :], AluOpType.max).then_inc(S["rd%d" % j], 1)
    ve.wait_ge(S.od, 1)
    if is_rank:
        ve.tensor_copy(T.ysend[:, QP:5 * QP], T.acc[:, QP:5 * QP]).then_inc(S.c1, 1)
        ve.tensor_copy(T.ysend[:, 5 * QP:SET], T.acc[:, 5 * QP:SET]).then_inc(S.c2, 1)
        ve.tensor_copy(T.ya[:, _cols(head, QP)], T.acc[:, 0:QP]).then_inc(S.y0, 1)
        early = _runs([(p - d) % NP for d in (0, 1, 2, 3)])
        late = _runs([(p - d) % NP for d in (4, 5)])
        ve.wait_ge(S.y0, 1)
        ve.wait_ge(S.arra1, 4 * (off // 4))
        ve.wait_ge(S.arrb1, 4 * (off // 4))
        for c in early:
            ve.tensor_tensor(T.yout[:, c], T.ya[:, c], T.yb[:, c], AluOpType.add).then_inc(S.yf1, 1)
        ve.wait_ge(S.arra2, off)
        ve.wait_ge(S.arrb2, 2 * (off // 2))
        for c in late:
            ve.tensor_tensor(T.yout[:, c], T.ya[:, c], T.yb[:, c], AluOpType.add).then_inc(S.yf2, 1)
        g.scalar.wait_ge(S.yf1, len(early))
        for c in early:
            g.scalar.dma_start(T.y[:, c], T.yout[:, c]).then_inc(S.st1, 16)
        g.scalar.wait_ge(S.st1, 16 * len(early))
        g.sync.wait_ge(S.yf2, len(late))
        for c in late:
            g.sync.dma_start(T.y[:, c], T.yout[:, c]).then_inc(S.st2, 16)
        g.sync.wait_ge(S.st2, 16 * len(late))
    else:
        ve.tensor_copy(T.ysend[:, 0:4 * QP], T.acc[:, 0:4 * QP]).then_inc(S.c1, 1)
        ve.tensor_copy(T.ysend[:, 4 * QP:SET], T.acc[:, 4 * QP:SET]).then_inc(S.c2, 1)
